import numpy as np
import ml_dtypes


def mxq(x, axis, fmt="e4m3"):
    dtype, down = {"e4m3": (ml_dtypes.float8_e4m3fn, 7), "e5m2": (ml_dtypes.float8_e5m2, 14)}[fmt]
    v = np.moveaxis(np.asarray(x, np.float32).astype(ml_dtypes.bfloat16).astype(np.float64), axis, -1)
    blocks = v.reshape(v.shape[:-1] + (-1, 32))
    amax = np.abs(blocks).max(-1, keepdims=True)
    byte = np.maximum(np.where(amax > 0, np.frexp(amax)[1] - 1 + 127, 0) - down, 1)
    scale = np.exp2(byte - 127.0)
    codes = (blocks / scale).astype(np.float32).astype(dtype).astype(np.float64)
    return np.moveaxis((codes * scale).reshape(v.shape), -1, axis)


WIDE = False


def mx_kscale(k):
    if not WIDE:
        return np.ones(k)
    levels = np.array([10, -10, 5, -5, 0])
    if k % 512:
        return np.exp2(np.random.permutation(np.resize(levels, k // 32))).repeat(32)
    a = np.empty((k // 512, 16))
    for p in range(k // 512):
        a[p, :8] = np.random.permutation(np.resize(levels, 8))
        for g in range(8):
            far = levels[np.abs(levels - a[p, g]) >= 10]
            a[p, g + 8] = far[np.random.randint(len(far))]
    return np.exp2(a.ravel()).repeat(32)


def f64(x):
    return np.asarray(x).astype(np.float64)


def striped(idx):
    return np.tile(idx.reshape(-1, 16).T, (8, 1)).astype(np.uint16)


def unstriped(offs):
    return offs[:16].T.reshape(-1).astype(np.int64)


def pack_weight(w):
    k, n = w.shape
    w = f64(np.asarray(w, np.float32).astype(ml_dtypes.bfloat16)).reshape(k // 32, 32, n)
    amax = np.abs(w).max(1)
    byte = np.clip(np.where(amax > 0, np.frexp(amax)[1] - 1 + 127 - 7, 1), 1, 254)
    scaled = (w * np.exp2(127.0 - byte)[:, None, :]).reshape(k, n).astype(np.float32)
    words = np.ascontiguousarray(scaled.reshape(k // 512, 128, 4, n).transpose(0, 1, 3, 2)).astype(ml_dtypes.float8_e4m3fn).view(np.uint8)
    return words, np.ascontiguousarray(byte.astype(np.uint8).reshape(k // 512, 16, n))


def unpack_weight(words, scales):
    g, p, n, _ = words.shape
    vals = np.ascontiguousarray(words).view(ml_dtypes.float8_e4m3fn).astype(np.float64) * np.repeat(np.exp2(scales.astype(np.float64) - 127.0), 8, axis=1)[..., None]
    return vals.transpose(0, 1, 3, 2).reshape(g * 512, n)


K, T, E, C, N = 1024, 512, 6, 256, 512
TOP = 3


def by_expert(wq, xq):
    return np.concatenate([wq[e].T @ xq[:, e * C:(e + 1) * C] for e in range(E)], axis=1)


def setup_inputs():
    n = np.random.standard_normal
    s = mx_kscale(K)[:, None]
    deal = np.repeat(np.arange(E), C).reshape(TOP, T)[:, np.random.permutation(T)]
    deal = np.take_along_axis(deal, np.argsort(np.random.rand(TOP, T), axis=0), axis=0)
    for _ in range(8):
        s_, t_ = np.random.permutation(T).reshape(2, -1); r = np.random.randint(TOP, size=T // 2); x, y = deal[r, s_].copy(), deal[r, t_].copy()
        ok = ~((deal[:, s_] == y).any(0) | (deal[:, t_] == x).any(0)); deal[r[ok], s_[ok]] = y[ok]; deal[r[ok], t_[ok]] = x[ok]
    order = np.lexsort((np.random.rand(TOP * T), deal.reshape(-1)))
    slot_token = order % T; pos = np.empty(TOP * T, np.int64); pos[order] = np.arange(TOP * T); pos = pos.reshape(TOP, T)
    g = np.random.uniform(0.5, 1.5, (TOP, T)); g = g / g.sum(0)
    packed = [pack_weight(m) for m in n((E, K, N)) / np.sqrt(K) / s[None]]
    w_slot = np.empty(E * C)
    for r in range(TOP): w_slot[pos[r]] = g[r]
    return {
        "xT": (n((K, T)) * s).astype(np.float32),
        "w_words": np.stack([m[0] for m in packed]),
        "w_scales": np.stack([m[1] for m in packed]),
        "gate": np.tile(w_slot, (K, 1)).astype(np.float32),
        "offs": striped(slot_token),
        "pos1": striped(pos[0]),
        "pos2": striped(pos[1]),
        "pos3": striped(pos[2]),
    }


def reference(xT, w_words, w_scales, gate, offs, pos1, pos2, pos3):
    idx = unstriped(offs)
    w = np.stack([unpack_weight(w_words[e], w_scales[e]) for e in range(E)])
    xq = mxq(f64(gate) * f64(xT)[:, idx], 0, "e4m3")
    y = by_expert(w, xq)
    return y[:, unstriped(pos1)] + y[:, unstriped(pos2)] + y[:, unstriped(pos3)]

@@ -1,0 +1,124 @@
+from contextlib import ExitStack
+
+import concourse.mybir as mybir
+
+K, T, E, C, N = 1024, 512, 6, 256, 512
+SLOTS = E * C
+FLOPS = 2 * K * N * SLOTS
+BYTES = 4 * K * T + E * K * N + E * (K // 32) * N + 4 * SLOTS + 2 * 128 * (SLOTS + 3 * T) // 16 + 4 * N * T
+
+F32 = mybir.dt.float32
+BF16 = mybir.dt.bfloat16
+I32 = mybir.dt.int32
+U32 = mybir.dt.uint32
+U16 = mybir.dt.uint16
+U8 = mybir.dt.uint8
+FP8X4 = mybir.dt.float8_e4m3fn_x4
+MULT = mybir.AluOpType.mult
+ADD = mybir.AluOpType.add
+
+P = 128
+PACK = 4
+K_PASS = P * PACK
+PASSES = K // K_PASS
+ROW_BLOCKS = N // P
+STRIPE = 16
+CHUNKS = (384, 384, 384, 256, 128)
+
+
+def runs(start, size, border):
+    cuts = [start] + [b for b in range(border, start + size, border) if b > start] + [start + size]
+    return list(zip(cuts[:-1], cuts[1:]))
+
+
+def tile_moe_pre_lin_none_kernel(tc, xT, w_words, w_scales, gate, offs, pos1, pos2, pos3, out):
+    nc = tc.nc
+    starts = [sum(CHUNKS[:c]) for c in range(len(CHUNKS))]
+
+    with ExitStack() as ctx:
+        keep = ctx.enter_context(tc.tile_pool(name="keep", bufs=1))
+        ring = ctx.enter_context(tc.tile_pool(name="ring", bufs=3))
+        psum = ctx.enter_context(tc.psum_pool(name="psum", bufs=2))
+
+        slot_token = keep.tile([P, SLOTS // STRIPE], U16, name="slot_token")
+        nc.sync.dma_start(slot_token[:], offs)
+
+        gates = [keep.tile([P, size], F32, name=f"gate{c}") for c, size in enumerate(CHUNKS)]
+        nc.sync.dma_start(gates[0][:], gate[0:P, 0:CHUNKS[0]])
+
+        x_rows = xT.rearrange("(a p j) t -> a j p t", a=PASSES, j=PACK)
+        planes = [[keep.tile([P, T], F32, name=f"x{a}_{j}") for j in range(PACK)] for a in range(PASSES)]
+        for a in range(PASSES):
+            for j in range(PACK):
+                nc.sync.dma_start(planes[a][j][:], x_rows[a, j])
+        for c in range(1, len(CHUNKS)):
+            nc.sync.dma_start(gates[c][:], gate[0:P, starts[c]:starts[c] + CHUNKS[c]])
+
+        w_planes = keep.tile([P, E * PASSES, N], U8, name="w_planes", align_bytes=64)
+        nc.vector.memset(w_planes[:].rearrange("p g n -> p (g n)").bitcast(I32), 0)
+        scale_rows = w_scales.rearrange("e a (q r) n -> r q (e a) n", r=4)
+        for r in range(4):
+            nc.sync.dma_start(w_planes[r:P:32, :, :].bitcast(I32), scale_rows[r].bitcast(I32))
+
+        w_codes = [keep.tile([P, PASSES, N], I32, name=f"w{e}", align_bytes=64) for e in range(E)]
+        for e in range(E):
+            nc.sync.dma_start(w_codes[e][:], w_words[e].rearrange("a p n r -> p a (n r)").bitcast(I32))
+
+        token_slots = []
+        for r, pos in enumerate((pos1, pos2, pos3)):
+            listed = keep.tile([P, T // STRIPE], U16, name=f"token_slot{r}")
+            nc.sync.dma_start(listed[:], pos)
+            token_slots.append(listed)
+
+        y = [keep.tile([P, SLOTS], F32, name=f"y{b}") for b in range(ROW_BLOCKS)]
+
+        for c, size in enumerate(CHUNKS):
+            start = starts[c]
+            offsets = slot_token[:, start // STRIPE:(start + size) // STRIPE]
+            codes, scales = [], []
+            for a in range(PASSES):
+                gated = ring.tile([P, PACK, size], F32, name="gated")
+                for j in range(PACK):
+                    nc.vector.tensor_tensor(gated[:, j, :], planes[a][j][:].indirect(offsets), gates[c][:], MULT)
+                grouped = ring.tile([P, size, PACK], BF16, name="grouped", align_bytes=64)
+                nc.scalar.copy(grouped[:], gated[:].rearrange("p j s -> p s j"))
+                x_codes = keep.tile([P, size], U32, name=f"x_codes{c}_{a}", align_bytes=64)
+                x_scales = keep.tile([P, size], U8, name=f"x_scales{c}_{a}", align_bytes=64)
+                for lo, hi in runs(0, size, C):
+                    nc.vector.quantize_mx(
+                        out=x_codes[:, lo:hi].bitcast(FP8X4),
+                        scales=x_scales[:, lo:hi],
+                        in_=grouped[:, lo:hi, :].rearrange("p s j -> p (s j)"),
+                    )
+                codes.append(x_codes)
+                scales.append(x_scales)
+            for b in range(ROW_BLOCKS):
+                cols = slice(b * P, (b + 1) * P)
+                acc = psum.tile([P, 512], F32, name=f"acc{b}")
+                for lo, hi in runs(start, size, C):
+                    e = lo // C
+                    own = slice(lo - start, hi - start)
+                    for a in range(PASSES):
+                        nc.tensor.matmul_mx(
+                            out=acc[:, own],
+                            lhsT=w_codes[e][:, a, cols].bitcast(FP8X4),
+                            lhsT_scale=w_planes[:, e * PASSES + a, cols],
+                            rhs=codes[a][:, own].bitcast(FP8X4),
+                            rhs_scale=scales[a][:, own],
+                            start=(a == 0),
+                            stop=(a == PASSES - 1),
+                        )
+                nc.scalar.copy(y[b][:, start:start + size], acc[:, 0:size])
+
+        for pair in range(0, ROW_BLOCKS, 2):
+            blocks = (pair, pair + 1)
+            first = {b: keep.tile([P, T], F32, name=f"first{b}") for b in blocks}
+            second = {b: keep.tile([P, T], F32, name=f"second{b}") for b in blocks}
+            total = {b: keep.tile([P, T], F32, name=f"total{b}") for b in blocks}
+            for b in blocks:
+                nc.vector.tensor_copy(first[b][:], y[b][:].indirect(token_slots[0][:]))
+            for b in blocks:
+                nc.vector.tensor_tensor(second[b][:], y[b][:].indirect(token_slots[1][:]), first[b][:], ADD)
+            for b in blocks:
+                nc.vector.tensor_tensor(total[b][:], y[b][:].indirect(token_slots[2][:]), second[b][:], ADD)
+                nc.sync.dma_start(out[b * P:(b + 1) * P, :], total[b][:])

@@ -23,36 +23,44 @@ K_PASS = P * PACK
 PASSES = K // K_PASS
 ROW_BLOCKS = N // P
 STRIPE = 16
-CHUNKS = (384, 384, 384, 256, 128)
+BANK = 512
+GATE_LOADS = (256, 512, 768,)
+STEPS = ((1536,), (768, 384, 256, 128,))
+LAST_STORES = (384, 128,)
 
 
-def runs(start, size, border):
-    cuts = [start] + [b for b in range(border, start + size, border) if b > start] + [start + size]
+def spans(sizes, start=0):
+    return [(start + sum(sizes[:i]), start + sum(sizes[:i + 1])) for i in range(len(sizes))]
+
+
+def runs(lo, hi, border):
+    cuts = [lo] + [b for b in range(border, hi, border) if b > lo] + [hi]
     return list(zip(cuts[:-1], cuts[1:]))
 
 
 def tile_moe_pre_lin_none_kernel(tc, xT, w_words, w_scales, gate, offs, pos1, pos2, pos3, out):
     nc = tc.nc
-    starts = [sum(CHUNKS[:c]) for c in range(len(CHUNKS))]
 
     with ExitStack() as ctx:
         keep = ctx.enter_context(tc.tile_pool(name="keep", bufs=1))
-        ring = ctx.enter_context(tc.tile_pool(name="ring", bufs=3))
-        psum = ctx.enter_context(tc.psum_pool(name="psum", bufs=2))
-
-        slot_token = keep.tile([P, SLOTS // STRIPE], U16, name="slot_token")
-        nc.sync.dma_start(slot_token[:], offs)
-
-        gates = [keep.tile([P, size], F32, name=f"gate{c}") for c, size in enumerate(CHUNKS)]
-        nc.sync.dma_start(gates[0][:], gate[0:P, 0:CHUNKS[0]])
+        psum = ctx.enter_context(tc.psum_pool(name="psum", bufs=1))
 
         x_rows = xT.rearrange("(a p j) t -> a j p t", a=PASSES, j=PACK)
-        planes = [[keep.tile([P, T], F32, name=f"x{a}_{j}") for j in range(PACK)] for a in range(PASSES)]
+        planes = [
+            [keep.tile([P, max(T, max(STEPS[a]) + 32)], F32, name=f"x{a}_{j}") for j in range(PACK)]
+            for a in range(PASSES)
+        ]
+        slot_token = keep.tile([P, SLOTS // STRIPE], U16, name="slot_token")
+        slot_gate = keep.tile([P, SLOTS], F32, name="slot_gate")
+
+        nc.sync.dma_start(planes[0][0][:, 0:T], x_rows[0, 0])
+        nc.sync.dma_start(slot_token[:], offs)
+        for lo, hi in spans(GATE_LOADS):
+            nc.sync.dma_start(slot_gate[:, lo:hi], gate[0:P, lo:hi])
         for a in range(PASSES):
             for j in range(PACK):
-                nc.sync.dma_start(planes[a][j][:], x_rows[a, j])
-        for c in range(1, len(CHUNKS)):
-            nc.sync.dma_start(gates[c][:], gate[0:P, starts[c]:starts[c] + CHUNKS[c]])
+                if (a, j) != (0, 0):
+                    nc.sync.dma_start(planes[a][j][:, 0:T], x_rows[a, j])
 
         w_planes = keep.tile([P, E * PASSES, N], U8, name="w_planes", align_bytes=64)
         nc.vector.memset(w_planes[:].rearrange("p g n -> p (g n)").bitcast(I32), 0)
@@ -70,45 +78,85 @@ def tile_moe_pre_lin_none_kernel(tc, xT, w_words, w_scales, gate, offs, pos1, po
             nc.sync.dma_start(listed[:], pos)
             token_slots.append(listed)
 
-        y = [keep.tile([P, SLOTS], F32, name=f"y{b}") for b in range(ROW_BLOCKS)]
+        x_codes = [keep.tile([P, SLOTS], U32, name=f"x_codes{a}", align_bytes=64) for a in range(PASSES)]
+        x_scales = [keep.tile([P, SLOTS], U8, name=f"x_scales{a}", align_bytes=64) for a in range(PASSES)]
 
-        for c, size in enumerate(CHUNKS):
-            start = starts[c]
-            offsets = slot_token[:, start // STRIPE:(start + size) // STRIPE]
-            codes, scales = [], []
-            for a in range(PASSES):
-                gated = ring.tile([P, PACK, size], F32, name="gated")
-                for j in range(PACK):
-                    nc.vector.tensor_tensor(gated[:, j, :], planes[a][j][:].indirect(offsets), gates[c][:], MULT)
-                grouped = ring.tile([P, size, PACK], BF16, name="grouped", align_bytes=64)
-                nc.scalar.copy(grouped[:], gated[:].rearrange("p j s -> p s j"))
-                x_codes = keep.tile([P, size], U32, name=f"x_codes{c}_{a}", align_bytes=64)
-                x_scales = keep.tile([P, size], U8, name=f"x_scales{c}_{a}", align_bytes=64)
-                for lo, hi in runs(0, size, C):
-                    nc.vector.quantize_mx(
-                        out=x_codes[:, lo:hi].bitcast(FP8X4),
-                        scales=x_scales[:, lo:hi],
-                        in_=grouped[:, lo:hi, :].rearrange("p s j -> p (s j)"),
+        steps = [(a, start, end) for a in range(PASSES) for start, end in spans(STEPS[a])]
+        last = len(steps) - 1
+
+        def staged(place, shape, dtype, name):
+            return keep.tile(shape, dtype, name=name, tag=f"stage{place % 3}", align_bytes=64)
+
+        def gather(s):
+            a, start, end = steps[s]
+            gated = staged(2 * s, [P, PACK, end - start], F32, f"gated{s}")
+            for j in range(PACK):
+                for lo, hi in spans(GATE_LOADS) if (s, j) == (0, 0) else [(start, end)]:
+                    window = planes[a][j][:].indirect(slot_token[:, lo // STRIPE:hi // STRIPE])
+                    nc.vector.tensor_tensor(gated[:, j, lo - start:hi - start], window, slot_gate[:, lo:hi], MULT)
+
+            grouped = staged(2 * s + 1, [P, end - start, PACK], BF16, f"grouped{s}")
+            copy = nc.vector.tensor_copy if s == last else nc.scalar.copy
+            for lo, hi in spans([w for w in (1024, 512, 256, 128) if (end - start) & w]):
+                copy(
+                    grouped[:, lo:hi, :].rearrange("p (s i) j -> p s j i", i=4),
+                    gated[:, :, lo:hi].rearrange("p j (s i) -> p s j i", i=4),
+                )
+            return grouped
+
+        def quantise(s, grouped):
+            a, start, end = steps[s]
+            for lo, hi in spans([w for w in (1024, 512, 256, 128) if (end - start) & w]):
+                nc.vector.quantize_mx(
+                    out=x_codes[a][:, start + lo:start + hi].bitcast(FP8X4),
+                    scales=x_scales[a][:, start + lo:start + hi],
+                    in_=grouped[:, lo:hi, :].rearrange("p s j -> p (s j)"),
+                )
+
+        def multiply(b, start, end, bank):
+            acc = psum.tile([P, BANK], F32, name=f"acc{b}_{start}", tag=f"bank{bank}")
+            cols = slice(b * P, (b + 1) * P)
+            for lo, hi in runs(start, end, C):
+                e = lo // C
+                for a in range(PASSES):
+                    nc.tensor.matmul_mx(
+                        out=acc[:, lo - start:hi - start],
+                        lhsT=w_codes[e][:, a, cols].bitcast(FP8X4),
+                        lhsT_scale=w_planes[:, e * PASSES + a, cols],
+                        rhs=x_codes[a][:, lo:hi].bitcast(FP8X4),
+                        rhs_scale=x_scales[a][:, lo:hi],
+                        start=(a == 0),
+                        stop=(a == PASSES - 1),
                     )
-                codes.append(x_codes)
-                scales.append(x_scales)
-            for b in range(ROW_BLOCKS):
-                cols = slice(b * P, (b + 1) * P)
-                acc = psum.tile([P, 512], F32, name=f"acc{b}")
-                for lo, hi in runs(start, size, C):
-                    e = lo // C
-                    own = slice(lo - start, hi - start)
-                    for a in range(PASSES):
-                        nc.tensor.matmul_mx(
-                            out=acc[:, own],
-                            lhsT=w_codes[e][:, a, cols].bitcast(FP8X4),
-                            lhsT_scale=w_planes[:, e * PASSES + a, cols],
-                            rhs=codes[a][:, own].bitcast(FP8X4),
-                            rhs_scale=scales[a][:, own],
-                            start=(a == 0),
-                            stop=(a == PASSES - 1),
-                        )
-                nc.scalar.copy(y[b][:, start:start + size], acc[:, 0:size])
+            return b, start, end, acc
+
+        def drain(copy, b, start, end, acc):
+            copy(y[b][:, start:end], acc[:, 0:end - start])
+
+        y = {b: keep.tile([P, SLOTS], F32, name=f"y{b}") for b in (0, 1)}
+        filled = []
+        used = 0
+        for s, (a, start, end) in enumerate(steps):
+            grouped = gather(s)
+            for piece in filled:
+                drain(nc.scalar.copy, *piece)
+            quantise(s, grouped)
+            filled = []
+            if a == PASSES - 1:
+                pieces = [(start + lo, start + hi) for lo, hi in runs(0, end - start, BANK)]
+                for b in (0, 1):
+                    for i, (lo, hi) in enumerate(pieces):
+                        filled.append(multiply(b, lo, hi, 3 * b + (used + i) % 3))
+                used = used + len(pieces)
+        for piece in filled:
+            drain(nc.vector.tensor_copy, *piece)
+
+        y[3] = staged(2 * last + 1, [P, SLOTS], F32, "y3")
+        y[2] = staged(2 * last, [P, SLOTS], F32, "y2")
+        late_banks = {3: (6, 7, 2), 2: (1, 4, 5)}
+        for i, (lo, hi) in enumerate(runs(0, SLOTS, BANK)):
+            for b in (3, 2):
+                drain(nc.scalar.copy, *multiply(b, lo, hi, late_banks[b][i]))
 
         for pair in range(0, ROW_BLOCKS, 2):
             blocks = (pair, pair + 1)
@@ -117,8 +165,11 @@ def tile_moe_pre_lin_none_kernel(tc, xT, w_words, w_scales, gate, offs, pos1, po
             total = {b: keep.tile([P, T], F32, name=f"total{b}") for b in blocks}
             for b in blocks:
                 nc.vector.tensor_copy(first[b][:], y[b][:].indirect(token_slots[0][:]))
+
             for b in blocks:
                 nc.vector.tensor_tensor(second[b][:], y[b][:].indirect(token_slots[1][:]), first[b][:], ADD)
             for b in blocks:
-                nc.vector.tensor_tensor(total[b][:], y[b][:].indirect(token_slots[2][:]), second[b][:], ADD)
-                nc.sync.dma_start(out[b * P:(b + 1) * P, :], total[b][:])
+                for lo, hi in spans(LAST_STORES if b == ROW_BLOCKS - 1 else (T,)):
+                    listed = token_slots[2][:, lo // STRIPE:hi // STRIPE]
+                    nc.vector.tensor_tensor(total[b][:, lo:hi], y[b][:].indirect(listed), second[b][:, lo:hi], ADD)
+                    nc.sync.dma_start(out[b * P:(b + 1) * P, lo:hi], total[b][:, lo:hi])

from contextlib import ExitStack

import concourse.mybir as mybir

K, T, E, C, N = 1024, 512, 6, 256, 512
SLOTS = E * C
FLOPS = 2 * K * N * SLOTS
BYTES = 4 * K * T + E * K * N + E * (K // 32) * N + 4 * SLOTS + 2 * 128 * (SLOTS + 3 * T) // 16 + 4 * N * T

F32 = mybir.dt.float32
BF16 = mybir.dt.bfloat16
I32 = mybir.dt.int32
U32 = mybir.dt.uint32
U16 = mybir.dt.uint16
U8 = mybir.dt.uint8
FP8X4 = mybir.dt.float8_e4m3fn_x4
MULT = mybir.AluOpType.mult
ADD = mybir.AluOpType.add

P = 128
PACK = 4
K_PASS = P * PACK
PASSES = K // K_PASS
ROW_BLOCKS = N // P
STRIPE = 16
BANK = 512
GATE_LOADS = (256, 512, 768,)
STEPS = ((1536,), (768, 384, 256, 128,))
LAST_STORES = (384, 128,)


def spans(sizes, start=0):
    return [(start + sum(sizes[:i]), start + sum(sizes[:i + 1])) for i in range(len(sizes))]


def runs(lo, hi, border):
    cuts = [lo] + [b for b in range(border, hi, border) if b > lo] + [hi]
    return list(zip(cuts[:-1], cuts[1:]))


def tile_moe_pre_lin_none_kernel(tc, xT, w_words, w_scales, gate, offs, pos1, pos2, pos3, out):
    nc = tc.nc

    with ExitStack() as ctx:
        keep = ctx.enter_context(tc.tile_pool(name="keep", bufs=1))
        psum = ctx.enter_context(tc.psum_pool(name="psum", bufs=1))

        x_rows = xT.rearrange("(a p j) t -> a j p t", a=PASSES, j=PACK)
        planes = [
            [keep.tile([P, max(T, max(STEPS[a]) + 32)], F32, name=f"x{a}_{j}") for j in range(PACK)]
            for a in range(PASSES)
        ]
        slot_token = keep.tile([P, SLOTS // STRIPE], U16, name="slot_token")
        slot_gate = keep.tile([P, SLOTS], F32, name="slot_gate")

        nc.sync.dma_start(planes[0][0][:, 0:T], x_rows[0, 0])
        nc.sync.dma_start(slot_token[:], offs)
        for lo, hi in spans(GATE_LOADS):
            nc.sync.dma_start(slot_gate[:, lo:hi], gate[0:P, lo:hi])
        for a in range(PASSES):
            for j in range(PACK):
                if (a, j) != (0, 0):
                    nc.sync.dma_start(planes[a][j][:, 0:T], x_rows[a, j])

        w_planes = keep.tile([P, E * PASSES, N], U8, name="w_planes", align_bytes=64)
        nc.vector.memset(w_planes[:].rearrange("p g n -> p (g n)").bitcast(I32), 0)
        scale_rows = w_scales.rearrange("e a (q r) n -> r q (e a) n", r=4)
        for r in range(4):
            nc.sync.dma_start(w_planes[r:P:32, :, :].bitcast(I32), scale_rows[r].bitcast(I32))

        w_codes = [keep.tile([P, PASSES, N], I32, name=f"w{e}", align_bytes=64) for e in range(E)]
        for e in range(E):
            nc.sync.dma_start(w_codes[e][:], w_words[e].rearrange("a p n r -> p a (n r)").bitcast(I32))

        token_slots = []
        for r, pos in enumerate((pos1, pos2, pos3)):
            listed = keep.tile([P, T // STRIPE], U16, name=f"token_slot{r}")
            nc.sync.dma_start(listed[:], pos)
            token_slots.append(listed)

        x_codes = [keep.tile([P, SLOTS], U32, name=f"x_codes{a}", align_bytes=64) for a in range(PASSES)]
        x_scales = [keep.tile([P, SLOTS], U8, name=f"x_scales{a}", align_bytes=64) for a in range(PASSES)]

        steps = [(a, start, end) for a in range(PASSES) for start, end in spans(STEPS[a])]
        last = len(steps) - 1

        def staged(place, shape, dtype, name):
            return keep.tile(shape, dtype, name=name, tag=f"stage{place % 3}", align_bytes=64)

        def gather(s):
            a, start, end = steps[s]
            gated = staged(2 * s, [P, PACK, end - start], F32, f"gated{s}")
            for j in range(PACK):
                for lo, hi in spans(GATE_LOADS) if (s, j) == (0, 0) else [(start, end)]:
                    window = planes[a][j][:].indirect(slot_token[:, lo // STRIPE:hi // STRIPE])
                    nc.vector.tensor_tensor(gated[:, j, lo - start:hi - start], window, slot_gate[:, lo:hi], MULT)

            grouped = staged(2 * s + 1, [P, end - start, PACK], BF16, f"grouped{s}")
            copy = nc.vector.tensor_copy if s == last else nc.scalar.copy
            for lo, hi in spans([w for w in (1024, 512, 256, 128) if (end - start) & w]):
                copy(
                    grouped[:, lo:hi, :].rearrange("p (s i) j -> p s j i", i=4),
                    gated[:, :, lo:hi].rearrange("p j (s i) -> p s j i", i=4),
                )
            return grouped

        def quantise(s, grouped):
            a, start, end = steps[s]
            for lo, hi in spans([w for w in (1024, 512, 256, 128) if (end - start) & w]):
                nc.vector.quantize_mx(
                    out=x_codes[a][:, start + lo:start + hi].bitcast(FP8X4),
                    scales=x_scales[a][:, start + lo:start + hi],
                    in_=grouped[:, lo:hi, :].rearrange("p s j -> p (s j)"),
                )

        def multiply(b, start, end, bank):
            acc = psum.tile([P, BANK], F32, name=f"acc{b}_{start}", tag=f"bank{bank}")
            cols = slice(b * P, (b + 1) * P)
            for lo, hi in runs(start, end, C):
                e = lo // C
                for a in range(PASSES):
                    nc.tensor.matmul_mx(
                        out=acc[:, lo - start:hi - start],
                        lhsT=w_codes[e][:, a, cols].bitcast(FP8X4),
                        lhsT_scale=w_planes[:, e * PASSES + a, cols],
                        rhs=x_codes[a][:, lo:hi].bitcast(FP8X4),
                        rhs_scale=x_scales[a][:, lo:hi],
                        start=(a == 0),
                        stop=(a == PASSES - 1),
                    )
            return b, start, end, acc

        def drain(copy, b, start, end, acc):
            copy(y[b][:, start:end], acc[:, 0:end - start])

        y = {b: keep.tile([P, SLOTS], F32, name=f"y{b}") for b in (0, 1)}
        filled = []
        used = 0
        for s, (a, start, end) in enumerate(steps):
            grouped = gather(s)
            for piece in filled:
                drain(nc.scalar.copy, *piece)
            quantise(s, grouped)
            filled = []
            if a == PASSES - 1:
                pieces = [(start + lo, start + hi) for lo, hi in runs(0, end - start, BANK)]
                for b in (0, 1):
                    for i, (lo, hi) in enumerate(pieces):
                        filled.append(multiply(b, lo, hi, 3 * b + (used + i) % 3))
                used = used + len(pieces)
        for piece in filled:
            drain(nc.vector.tensor_copy, *piece)

        y[3] = staged(2 * last + 1, [P, SLOTS], F32, "y3")
        y[2] = staged(2 * last, [P, SLOTS], F32, "y2")
        late_banks = {3: (6, 7, 2), 2: (1, 4, 5)}
        for i, (lo, hi) in enumerate(runs(0, SLOTS, BANK)):
            for b in (3, 2):
                drain(nc.scalar.copy, *multiply(b, lo, hi, late_banks[b][i]))

        for pair in range(0, ROW_BLOCKS, 2):
            blocks = (pair, pair + 1)
            first = {b: keep.tile([P, T], F32, name=f"first{b}") for b in blocks}
            second = {b: keep.tile([P, T], F32, name=f"second{b}") for b in blocks}
            total = {b: keep.tile([P, T], F32, name=f"total{b}") for b in blocks}
            for b in blocks:
                nc.vector.tensor_copy(first[b][:], y[b][:].indirect(token_slots[0][:]))

            for b in blocks:
                nc.vector.tensor_tensor(second[b][:], y[b][:].indirect(token_slots[1][:]), first[b][:], ADD)
            for b in blocks:
                for lo, hi in spans(LAST_STORES if b == ROW_BLOCKS - 1 else (T,)):
                    listed = token_slots[2][:, lo // STRIPE:hi // STRIPE]
                    nc.vector.tensor_tensor(total[b][:, lo:hi], y[b][:].indirect(listed), second[b][:, lo:hi], ADD)
                    nc.sync.dma_start(out[b * P:(b + 1) * P, lo:hi], total[b][:, lo:hi])
